import numpy as np
import ml_dtypes


def mxq(x, axis, fmt="e4m3"):
    dtype, down = {"e4m3": (ml_dtypes.float8_e4m3fn, 7), "e5m2": (ml_dtypes.float8_e5m2, 14)}[fmt]
    v = np.moveaxis(np.asarray(x, np.float32).astype(ml_dtypes.bfloat16).astype(np.float64), axis, -1)
    blocks = v.reshape(v.shape[:-1] + (-1, 32))
    amax = np.abs(blocks).max(-1, keepdims=True)
    byte = np.maximum(np.where(amax > 0, np.frexp(amax)[1] - 1 + 127, 0) - down, 1)
    scale = np.exp2(byte - 127.0)
    codes = (blocks / scale).astype(np.float32).astype(dtype).astype(np.float64)
    return np.moveaxis((codes * scale).reshape(v.shape), -1, axis)


WIDE = False


def mx_kscale(k):
    if not WIDE:
        return np.ones(k)
    levels = np.array([30, -30])
    if k % 512:
        return np.exp2(np.random.permutation(np.resize(levels, k // 32))).repeat(32)
    a = np.empty((k // 512, 16))
    for p in range(k // 512):
        a[p, :8] = np.random.permutation(np.resize(levels, 8))
        for g in range(8):
            far = levels[np.abs(levels - a[p, g]) >= 10]
            a[p, g + 8] = far[np.random.randint(len(far))]
    return np.exp2(a.ravel()).repeat(32)


def f64(x):
    return np.asarray(x).astype(np.float64)


E2M1 = np.array([0.0, 0.5, 1.0, 1.5, 2.0, 3.0, 4.0, 6.0, -0.0, -0.5, -1.0, -1.5, -2.0, -3.0, -4.0, -6.0])


def pack_weight(w, fmt):
    k, n = w.shape
    w = f64(np.asarray(w, np.float32).astype(ml_dtypes.bfloat16)).reshape(k // 32, 32, n)
    amax = np.abs(w).max(1)
    if fmt == "e4m3":
        byte = np.frexp(amax)[1] - 1 + 127 - 7
    else:
        mant, ex = np.frexp(amax / 6.0)
        byte = np.where(mant > 0.5, ex, ex - 1) + 127
    byte = np.clip(np.where(amax > 0, byte, 1), 1, 254)
    scaled = (w * np.exp2(127.0 - byte)[:, None, :]).reshape(k, n).astype(np.float32)
    by_word = np.ascontiguousarray(scaled.reshape(k // 512, 128, 4, n).transpose(0, 1, 3, 2))
    if fmt == "e4m3":
        words = by_word.astype(ml_dtypes.float8_e4m3fn).view(np.uint8)
    else:
        c = by_word.astype(ml_dtypes.float4_e2m1fn).view(np.uint8) & 0xF
        words = (c[..., 0::2] | (c[..., 1::2] << 4)).reshape(k // 512, 128, 2 * n)
    return np.ascontiguousarray(words), np.ascontiguousarray(byte.astype(np.uint8).reshape(k // 512, 16, n))


def unpack_weight(words, scales, fmt):
    g, _, n = scales.shape
    words = np.ascontiguousarray(words).reshape(g, 128, n, -1)
    if fmt == "e4m3":
        vals = words.view(ml_dtypes.float8_e4m3fn).astype(np.float64)
    else:
        nib = np.empty((g, 128, n, 4), np.uint8)
        nib[..., 0::2] = words & 0xF
        nib[..., 1::2] = words >> 4
        vals = E2M1[nib]
    vals = vals * np.repeat(np.exp2(scales.astype(np.float64) - 127.0), 8, axis=1)[..., None]
    return vals.transpose(0, 1, 3, 2).reshape(g * 512, n)


def bf(x):
    return np.asarray(x, np.float32).astype(ml_dtypes.bfloat16)


def planes(Y):
    r, m = Y.shape
    b = f64(bf(Y)).reshape(r // 32, 32, m)
    amax = np.abs(b).max(1)
    byte = np.clip(np.where(amax > 0, np.frexp(amax)[1] - 1 + 127 - 7, 1), 1, 254)
    codes = (b * np.exp2(127.0 - byte)[:, None, :]).reshape(r, m).astype(np.float32).astype(ml_dtypes.float8_e4m3fn).view(np.uint8)
    words = codes.reshape(r // 512, 128, 4, m).transpose(0, 1, 3, 2)
    return np.ascontiguousarray(words), np.ascontiguousarray(byte.astype(np.uint8).reshape(r // 512, 16, m))


N, M, L, T, K = 512, 512, 1024, 512, 512


def setup_inputs():
    n = np.random.standard_normal
    fn = mx_kscale(N)
    fm = mx_kscale(M)
    fl = mx_kscale(L)
    wap = pack_weight(n((N, K)) * 1 / np.sqrt(N) * fn[:, None], "e4m3")
    wbp = pack_weight(n((M, K)) * 1 / np.sqrt(M) * fm[:, None], "e2m1")
    gcp = pack_weight(n((L, T)) / fl[:, None], "e4m3")
    wcp = pack_weight(n((L, K)) * 1 / np.sqrt(L) * fl[:, None], "e2m1")
    return {
        "ga": (n((N, T)) * np.exp(0.5 * n((1, T))) / fn[:, None]).astype(np.float32),
        "wa_words": wap[0],
        "wa_scales": wap[1],
        "gb": (n((M, T)) / fm[:, None]).astype(np.float32),
        "wb_words": wbp[0],
        "wb_scales": wbp[1],
        "gc_words": gcp[0],
        "gc_scales": gcp[1],
        "wc_words": wcp[0],
        "wc_scales": wcp[1],
        "fo": (np.random.uniform(0.5, 2.0, (K, 1))).astype(np.float32),
    }


def reference(ga, wa_words, wa_scales, gb, wb_words, wb_scales, gc_words, gc_scales, wc_words, wc_scales, fo):
    wau = unpack_weight(wa_words, wa_scales, "e4m3")
    wbu = unpack_weight(wb_words, wb_scales, "e2m1")
    gcu = unpack_weight(gc_words, gc_scales, "e4m3")
    wcu = unpack_weight(wc_words, wc_scales, "e2m1")
    gaq = mxq(f64(ga), 0, "e5m2")
    gbq = mxq(f64(gb), 0, "e4m3")
    p = wau.T @ gaq + wbu.T @ gbq + wcu.T @ gcu
    y = p * f64(fo)
    words, scales = planes(y)
    return y, words, scales

@@ -1,0 +1,179 @@
+from contextlib import ExitStack
+
+import concourse.mybir as mybir
+
+F32 = mybir.dt.float32
+BF16 = mybir.dt.bfloat16
+I32 = mybir.dt.int32
+U32 = mybir.dt.uint32
+U8 = mybir.dt.uint8
+E4M3 = mybir.dt.float8_e4m3fn_x4
+E5M2 = mybir.dt.float8_e5m2_x4
+E2M1 = mybir.dt.float4_e2m1fn_x4
+
+P = 128
+PACK = 4
+T = 512
+K = 512
+HALF = T // 2
+NARROW = 128
+LINE = 4
+
+FLOPS = 2 * K * T * (512 + 512 + 1024)
+
+
+def load_scale_rows(queue, plane, scales):
+    for q in range(4):
+        queue.dma_start(
+            out=plane[32 * q : 32 * q + 4, :, :].bitcast(I32),
+            in_=scales[:, 4 * q : 4 * q + 4, :].rearrange("z r c -> r z c").bitcast(I32),
+        )
+
+
+def deal_scales(nc, dealt, raw):
+    nc.vector.tensor_copy(
+        out=dealt.rearrange("p z (r m) -> p z r m", r=PACK),
+        in_=raw.rearrange("p z (m r) -> p z r m", r=PACK),
+    )
+
+
+def deal_e2m1(nc, dealt, raw):
+    nc.vector.tensor_copy(
+        out=dealt.rearrange("p (r m b) -> p r m b", r=PACK, b=2),
+        in_=raw.rearrange("p (m r b) -> p r m b", r=PACK, b=2),
+    )
+
+
+def interleave(copy, grouped, rows):
+    copy(
+        out=grouped.rearrange("p (c i) j -> p c j i", i=LINE),
+        in_=rows.rearrange("p j (c i) -> p c j i", i=LINE),
+    )
+
+
+def quantize(nc, codes, scales, grouped, fmt):
+    nc.vector.quantize_mx(out=codes.bitcast(fmt), scales=scales, in_=grouped.rearrange("p c j -> p (c j)"))
+
+
+def tile_mix_gradient_of_three_branches_pl_kernel(
+    tc, ga, wa_words, wa_scales, gb, wb_words, wb_scales, gc_words, gc_scales, wc_words, wc_scales, fo,
+    out_0, out_1, out_2,
+):
+    nc = tc.nc
+    with ExitStack() as ctx:
+        sb = ctx.enter_context(tc.tile_pool(name="sb", bufs=1))
+        ps = ctx.enter_context(tc.psum_pool(name="ps", bufs=1))
+        ctx.enter_context(tc.manual_schedule())
+
+        wc_raw = sb.tile([P, 2, 2 * K], U8, align_bytes=64)
+        wb_raw = sb.tile([P, 2 * K], U8, align_bytes=64)
+        wa_raw = sb.tile([P, K], U32, align_bytes=64)
+        wc_s_raw = sb.tile([P, 2, K], U8, align_bytes=64)
+        wb_s_raw = sb.tile([P, 1, K], U8, align_bytes=64)
+        wa_s_raw = sb.tile([P, 1, K], U8, align_bytes=64)
+        wc_codes = sb.tile([P, 2, 2 * K], U8, align_bytes=64)
+        wb_codes = sb.tile([P, 2 * K], U8, align_bytes=64)
+        wa_codes = sb.tile([P, K], U32, align_bytes=64)
+        wc_s = sb.tile([P, 2, K], U8, align_bytes=64)
+        wb_s = sb.tile([P, 1, K], U8, align_bytes=64)
+        wa_s = sb.tile([P, 1, K], U8, align_bytes=64)
+        gc_codes = sb.tile([P, 2, T], U32, align_bytes=64)
+        gc_s = sb.tile([P, 2, T], U8, align_bytes=64)
+        ga_raw = sb.tile([P, PACK, T], F32, align_bytes=64)
+        gb_raw = [sb.tile([P, PACK, HALF], F32, align_bytes=64, name="gb_raw%d" % h) for h in range(2)]
+        ga_bf = [sb.tile([P, HALF, PACK], BF16, align_bytes=64, name="ga_bf%d" % h) for h in range(2)]
+        gb_bf = [sb.tile([P, HALF, PACK], BF16, align_bytes=64, name="gb_bf%d" % h) for h in range(2)]
+        y_bf = [sb.tile([P, HALF, PACK], BF16, align_bytes=64, name="y_bf%d" % h) for h in range(2)]
+        ga_codes = sb.tile([P, T], U32, align_bytes=64)
+        ga_s = sb.tile([P, T], U8, align_bytes=64)
+        gb_codes = sb.tile([P, T], U32, align_bytes=64)
+        gb_s = sb.tile([P, T], U8, align_bytes=64)
+        y_codes = sb.tile([P, T], U32, align_bytes=64)
+        y_s = sb.tile([P, T], U8, align_bytes=64)
+        y = sb.tile([P, PACK, T], F32, align_bytes=64)
+        fo_sb = sb.tile([P, PACK], F32, align_bytes=64)
+        acc = [ps.tile([P, T], F32, name="acc%d" % r) for r in range(PACK)]
+
+        halves = [slice(0, HALF), slice(HALF, T)]
+
+        for plane in (wc_s_raw, gc_s, wb_s_raw):
+            nc.vector.memset(plane[:].bitcast(I32), 0)
+        nc.gpsimd.memset(wa_s_raw[:].bitcast(I32), 0)
+        load_scale_rows(nc.gpsimd, wa_s_raw, wa_scales)
+
+        gb_rows = gb.rearrange("(p j) t -> p j t", j=PACK)
+        nc.sync.dma_start(out=wc_raw[:].bitcast(I32), in_=wc_words.rearrange("z p b -> p z b").bitcast(I32))
+        load_scale_rows(nc.sync, wc_s_raw, wc_scales)
+        nc.sync.dma_start(out=gc_codes[:].bitcast(I32), in_=gc_words.rearrange("z p c r -> p z (c r)").bitcast(I32))
+        nc.sync.dma_start(out=wa_raw[:].bitcast(I32), in_=wa_words[0].rearrange("p c r -> p (c r)").bitcast(I32))
+        nc.sync.dma_start(out=wb_raw[:].bitcast(I32), in_=wb_words[0].bitcast(I32))
+        load_scale_rows(nc.sync, gc_s, gc_scales)
+        nc.sync.dma_start(out=ga_raw[:], in_=ga.rearrange("(p j) t -> p j t", j=PACK))
+        load_scale_rows(nc.sync, wb_s_raw, wb_scales)
+        nc.sync.dma_start(out=gb_raw[0][:], in_=gb_rows[:, :, halves[0]])
+        nc.sync.dma_start(out=fo_sb[:], in_=fo.rearrange("(p r) o -> p (r o)", r=PACK))
+        nc.sync.dma_start(out=gb_raw[1][:], in_=gb_rows[:, :, halves[1]])
+
+        def multiply(r, w_codes, w_s, g_codes, g_s, cols, start, stop):
+            nc.tensor.matmul_mx(
+                out=acc[r][:, cols], lhsT=w_codes, lhsT_scale=w_s[:, r * P : (r + 1) * P],
+                rhs=g_codes, rhs_scale=g_s, start=start, stop=stop,
+            )
+
+        for z in range(2):
+            deal_e2m1(nc, wc_codes[:, z, :], wc_raw[:, z, :])
+        deal_scales(nc, wc_s[:], wc_s_raw[:])
+        for z in range(2):
+            for r in range(PACK):
+                multiply(r, wc_codes[:, z, 2 * P * r : 2 * P * (r + 1)].bitcast(E2M1), wc_s[:, z, :],
+                         gc_codes[:, z, :].bitcast(E4M3), gc_s[:, z, :], slice(0, T), z == 0, False)
+
+        nc.vector.tensor_copy(
+            out=wa_codes[:].bitcast(I32).rearrange("p (r g i) -> p g r i", r=PACK, i=LINE),
+            in_=wa_raw[:].bitcast(I32).rearrange("p (g i r) -> p g r i", r=PACK, i=LINE),
+        )
+        deal_scales(nc, wa_s[:], wa_s_raw[:])
+        deal_e2m1(nc, wb_codes[:], wb_raw[:])
+
+        def round_wide(rows, grouped, share):
+            interleave(nc.scalar.copy, grouped[0][:, :share, :], rows[:, :, :share])
+            interleave(nc.vector.tensor_copy, grouped[1][:], rows[:, :, halves[1]])
+            interleave(nc.vector.tensor_copy, grouped[0][:, share:, :], rows[:, :, share:HALF])
+
+        round_wide(ga_raw, ga_bf, 192)
+        for h in (1, 0):
+            quantize(nc, ga_codes[:, halves[h]], ga_s[:, halves[h]], ga_bf[h][:], E5M2)
+        for r in range(PACK):
+            multiply(r, wa_codes[:, r * P : (r + 1) * P].bitcast(E4M3), wa_s[:, 0, :],
+                     ga_codes[:].bitcast(E5M2), ga_s[:], slice(0, T), False, False)
+
+        deal_scales(nc, wb_s[:], wb_s_raw[:])
+        for h in range(2):
+            share = 128 if h == 0 else 96
+            interleave(nc.scalar.copy, gb_bf[h][:, :share, :], gb_raw[h][:, :, :share])
+            interleave(nc.vector.tensor_copy, gb_bf[h][:, share:, :], gb_raw[h][:, :, share:])
+            quantize(nc, gb_codes[:, halves[h]], gb_s[:, halves[h]], gb_bf[h][:], E4M3)
+            for r in range(PACK):
+                for c0 in range(h * HALF, (h + 1) * HALF, NARROW):
+                    cols = slice(c0, c0 + NARROW)
+                    multiply(r, wb_codes[:, 2 * P * r : 2 * P * (r + 1)].bitcast(E2M1), wb_s[:, 0, :],
+                             gb_codes[:, cols].bitcast(E4M3), gb_s[:, cols], cols, False, c0 + NARROW == T)
+
+        out_rows = out_0.rearrange("(p r) t -> p r t", r=PACK)
+        for r in range(PACK):
+            if r % 2 == 0:
+                nc.scalar.activation(out=y[:, r, :], in_=acc[r][:], func=mybir.ActivationFunctionType.Copy,
+                                     scale=fo_sb[:, r : r + 1])
+            else:
+                nc.vector.tensor_scalar(out=y[:, r, :], in0=acc[r][:], scalar1=fo_sb[:, r : r + 1], scalar2=None,
+                                        op0=mybir.AluOpType.mult)
+            nc.sync.dma_start(out=out_rows[:, r, :], in_=y[:, r, :])
+        round_wide(y, y_bf, 192)
+        words = out_1[0].rearrange("p c r -> p (c r)").bitcast(I32)
+        for h in (1, 0):
+            quantize(nc, y_codes[:, halves[h]], y_s[:, halves[h]], y_bf[h][:], E4M3)
+            nc.sync.dma_start(out=words[:, halves[h]], in_=y_codes[:, halves[h]].bitcast(I32))
+        for q in range(4):
+            queue = nc.scalar if q % 2 == 0 else nc.sync
+            queue.dma_start(out=out_2[0, 4 * q : 4 * q + 4, :].bitcast(I32),
+                            in_=y_s[32 * q : 32 * q + 4, :].bitcast(I32))

@@ -23,11 +23,7 @@ FLOPS = 2 * K * T * (512 + 512 + 1024)
 
 
 def load_scale_rows(queue, plane, scales):
-    for q in range(4):
-        queue.dma_start(
-            out=plane[32 * q : 32 * q + 4, :, :].bitcast(I32),
-            in_=scales[:, 4 * q : 4 * q + 4, :].rearrange("z r c -> r z c").bitcast(I32),
-        )
+    queue.dma_start(out=plane.bitcast(I32), in_=scales.rearrange("z r c -> r z c").bitcast(I32))
 
 
 def deal_scales(nc, dealt, raw):
@@ -68,9 +64,12 @@ def tile_mix_gradient_of_three_branches_pl_kernel(
         wc_raw = sb.tile([P, 2, 2 * K], U8, align_bytes=64)
         wb_raw = sb.tile([P, 2 * K], U8, align_bytes=64)
         wa_raw = sb.tile([P, K], U32, align_bytes=64)
-        wc_s_raw = sb.tile([P, 2, K], U8, align_bytes=64)
-        wb_s_raw = sb.tile([P, 1, K], U8, align_bytes=64)
-        wa_s_raw = sb.tile([P, 1, K], U8, align_bytes=64)
+        planes = sb.tile([P, 6, K], U8, align_bytes=64)
+        staged = sb.tile([16, 6, K], U8, align_bytes=64)
+        wc_s_raw = planes[:, 0:2, :]
+        gc_s = planes[:, 2:4, :]
+        wa_s_raw = planes[:, 4:5, :]
+        wb_s_raw = planes[:, 5:6, :]
         wc_codes = sb.tile([P, 2, 2 * K], U8, align_bytes=64)
         wb_codes = sb.tile([P, 2 * K], U8, align_bytes=64)
         wa_codes = sb.tile([P, K], U32, align_bytes=64)
@@ -78,7 +77,6 @@ def tile_mix_gradient_of_three_branches_pl_kernel(
         wb_s = sb.tile([P, 1, K], U8, align_bytes=64)
         wa_s = sb.tile([P, 1, K], U8, align_bytes=64)
         gc_codes = sb.tile([P, 2, T], U32, align_bytes=64)
-        gc_s = sb.tile([P, 2, T], U8, align_bytes=64)
         ga_raw = sb.tile([P, PACK, T], F32, align_bytes=64)
         gb_raw = [sb.tile([P, PACK, HALF], F32, align_bytes=64, name="gb_raw%d" % h) for h in range(2)]
         ga_bf = [sb.tile([P, HALF, PACK], BF16, align_bytes=64, name="ga_bf%d" % h) for h in range(2)]
@@ -96,20 +94,21 @@ def tile_mix_gradient_of_three_branches_pl_kernel(
 
         halves = [slice(0, HALF), slice(HALF, T)]
 
-        for plane in (wc_s_raw, gc_s, wb_s_raw):
-            nc.vector.memset(plane[:].bitcast(I32), 0)
-        nc.gpsimd.memset(wa_s_raw[:].bitcast(I32), 0)
-        load_scale_rows(nc.gpsimd, wa_s_raw, wa_scales)
+        nc.vector.memset(planes[:].bitcast(I32), 0)
 
         gb_rows = gb.rearrange("(p j) t -> p j t", j=PACK)
+        load_scale_rows(nc.sync, staged[:, 0:2, :], wc_scales)
+        load_scale_rows(nc.sync, staged[:, 2:4, :], gc_scales)
+        load_scale_rows(nc.sync, staged[:, 4:5, :], wa_scales)
+        load_scale_rows(nc.sync, staged[:, 5:6, :], wb_scales)
         nc.sync.dma_start(out=wc_raw[:].bitcast(I32), in_=wc_words.rearrange("z p b -> p z b").bitcast(I32))
-        load_scale_rows(nc.sync, wc_s_raw, wc_scales)
         nc.sync.dma_start(out=gc_codes[:].bitcast(I32), in_=gc_words.rearrange("z p c r -> p z (c r)").bitcast(I32))
         nc.sync.dma_start(out=wa_raw[:].bitcast(I32), in_=wa_words[0].rearrange("p c r -> p (c r)").bitcast(I32))
         nc.sync.dma_start(out=wb_raw[:].bitcast(I32), in_=wb_words[0].bitcast(I32))
-        load_scale_rows(nc.sync, gc_s, gc_scales)
+        for q in range(4):
+            nc.sync.dma_start(out=planes[32 * q : 32 * q + 4, :, :].bitcast(I32),
+                              in_=staged[4 * q : 4 * q + 4, :, :].bitcast(I32))
         nc.sync.dma_start(out=ga_raw[:], in_=ga.rearrange("(p j) t -> p j t", j=PACK))
-        load_scale_rows(nc.sync, wb_s_raw, wb_scales)
         nc.sync.dma_start(out=gb_raw[0][:], in_=gb_rows[:, :, halves[0]])
         nc.sync.dma_start(out=fo_sb[:], in_=fo.rearrange("(p r) o -> p (r o)", r=PACK))
         nc.sync.dma_start(out=gb_raw[1][:], in_=gb_rows[:, :, halves[1]])
@@ -122,18 +121,19 @@ def tile_mix_gradient_of_three_branches_pl_kernel(
 
         for z in range(2):
             deal_e2m1(nc, wc_codes[:, z, :], wc_raw[:, z, :])
-        deal_scales(nc, wc_s[:], wc_s_raw[:])
-        for z in range(2):
-            for r in range(PACK):
-                multiply(r, wc_codes[:, z, 2 * P * r : 2 * P * (r + 1)].bitcast(E2M1), wc_s[:, z, :],
-                         gc_codes[:, z, :].bitcast(E4M3), gc_s[:, z, :], slice(0, T), z == 0, False)
-
         nc.vector.tensor_copy(
             out=wa_codes[:].bitcast(I32).rearrange("p (r g i) -> p g r i", r=PACK, i=LINE),
             in_=wa_raw[:].bitcast(I32).rearrange("p (g i r) -> p g r i", r=PACK, i=LINE),
         )
-        deal_scales(nc, wa_s[:], wa_s_raw[:])
         deal_e2m1(nc, wb_codes[:], wb_raw[:])
+        for z in range(2):
+            deal_scales(nc, wc_s[:, z : z + 1, :], wc_s_raw[:, z : z + 1, :])
+            for r in range(PACK):
+                multiply(r, wc_codes[:, z, 2 * P * r : 2 * P * (r + 1)].bitcast(E2M1), wc_s[:, z, :],
+                         gc_codes[:, z, :].bitcast(E4M3), gc_s[:, z, :], slice(0, T), z == 0, False)
+
+        deal_scales(nc, wa_s[:], wa_s_raw)
+        deal_scales(nc, wb_s[:], wb_s_raw)
 
         def round_wide(rows, grouped, share):
             interleave(nc.scalar.copy, grouped[0][:, :share, :], rows[:, :, :share])
@@ -147,7 +147,6 @@ def tile_mix_gradient_of_three_branches_pl_kernel(
             multiply(r, wa_codes[:, r * P : (r + 1) * P].bitcast(E4M3), wa_s[:, 0, :],
                      ga_codes[:].bitcast(E5M2), ga_s[:], slice(0, T), False, False)
 
-        deal_scales(nc, wb_s[:], wb_s_raw[:])
         for h in range(2):
             share = 128 if h == 0 else 96
             interleave(nc.scalar.copy, gb_bf[h][:, :share, :], gb_raw[h][:, :, :share])
@@ -160,16 +159,33 @@ def tile_mix_gradient_of_three_branches_pl_kernel(
                              gb_codes[:, cols].bitcast(E4M3), gb_s[:, cols], cols, False, c0 + NARROW == T)
 
         out_rows = out_0.rearrange("(p r) t -> p r t", r=PACK)
-        for r in range(PACK):
-            if r % 2 == 0:
-                nc.scalar.activation(out=y[:, r, :], in_=acc[r][:], func=mybir.ActivationFunctionType.Copy,
-                                     scale=fo_sb[:, r : r + 1])
-            else:
-                nc.vector.tensor_scalar(out=y[:, r, :], in0=acc[r][:], scalar1=fo_sb[:, r : r + 1], scalar2=None,
-                                        op0=mybir.AluOpType.mult)
+        def scale_on_scalar(r, cols):
+            nc.scalar.activation(out=y[:, r, cols], in_=acc[r][:, cols], func=mybir.ActivationFunctionType.Copy,
+                                 scale=fo_sb[:, r : r + 1])
+
+        def scale_on_vector(r, cols):
+            nc.vector.tensor_scalar(out=y[:, r, cols], in0=acc[r][:, cols], scalar1=fo_sb[:, r : r + 1], scalar2=None,
+                                    op0=mybir.AluOpType.mult)
+
+        def store_rows(r):
             nc.sync.dma_start(out=out_rows[:, r, :], in_=y[:, r, :])
-        round_wide(y, y_bf, 192)
+
+        whole = slice(0, T)
         words = out_1[0].rearrange("p c r -> p (c r)").bitcast(I32)
+        scale_on_scalar(0, whole)
+        store_rows(0)
+        scale_on_vector(1, whole)
+        store_rows(1)
+        scale_on_scalar(2, halves[1])
+        scale_on_vector(3, halves[1])
+        scale_on_scalar(2, halves[0])
+        store_rows(2)
+        scale_on_scalar(3, halves[0])
+        store_rows(3)
+        share = 192
+        interleave(nc.vector.tensor_copy, y_bf[1][:], y[:, :, halves[1]])
+        interleave(nc.scalar.copy, y_bf[0][:, :share, :], y[:, :, :share])
+        interleave(nc.vector.tensor_copy, y_bf[0][:, share:, :], y[:, :, share:HALF])
         for h in (1, 0):
             quantize(nc, y_codes[:, halves[h]], y_s[:, halves[h]], y_bf[h][:], E4M3)
             nc.sync.dma_start(out=words[:, halves[h]], in_=y_codes[:, halves[h]].bitcast(I32))

@@ -18,37 +18,56 @@ K = 512
 HALF = T // 2
 NARROW = 128
 LINE = 4
+BLOCKS = 16
+QUADRANT = 32
+STAGE = 16
+PLANES = 6
+
+SCALAR_COLUMNS_GB = 96
+SCALAR_COLUMNS_Y = 128
 
 FLOPS = 2 * K * T * (512 + 512 + 1024)
 
 
-def load_scale_rows(queue, plane, scales):
-    queue.dma_start(out=plane.bitcast(I32), in_=scales.rearrange("z r c -> r z c").bitcast(I32))
+def stage_scale_rows(queue, staged, scales):
+    queue.dma_start(out=staged.bitcast(I32), in_=scales.rearrange("z q c -> q z c").bitcast(I32))
 
 
-def deal_scales(nc, dealt, raw):
+def deal_plane(nc, dealt, arrived):
     nc.vector.tensor_copy(
-        out=dealt.rearrange("p z (r m) -> p z r m", r=PACK),
-        in_=raw.rearrange("p z (m r) -> p z r m", r=PACK),
+        out=dealt.rearrange("p (r m) -> p r m", r=PACK),
+        in_=arrived.rearrange("p (m r) -> p r m", r=PACK),
     )
 
 
-def deal_e2m1(nc, dealt, raw):
+def deal_e2m1(nc, dealt, arrived):
     nc.vector.tensor_copy(
         out=dealt.rearrange("p (r m b) -> p r m b", r=PACK, b=2),
-        in_=raw.rearrange("p (m r b) -> p r m b", r=PACK, b=2),
+        in_=arrived.rearrange("p (m r b) -> p r m b", r=PACK, b=2),
     )
 
 
-def interleave(copy, grouped, rows):
+def deal_e4m3(nc, dealt, arrived):
+    nc.vector.tensor_copy(
+        out=dealt.bitcast(I32).rearrange("p (r g i) -> p g r i", r=PACK, i=LINE),
+        in_=arrived.bitcast(I32).rearrange("p (g i r) -> p g r i", r=PACK, i=LINE),
+    )
+
+
+def round_and_interleave(copy, grouped, rows):
     copy(
         out=grouped.rearrange("p (c i) j -> p c j i", i=LINE),
         in_=rows.rearrange("p j (c i) -> p c j i", i=LINE),
     )
 
 
-def quantize(nc, codes, scales, grouped, fmt):
-    nc.vector.quantize_mx(out=codes.bitcast(fmt), scales=scales, in_=grouped.rearrange("p c j -> p (c j)"))
+def round_on_both_engines(nc, grouped, rows, scalar_columns):
+    round_and_interleave(nc.scalar.copy, grouped[:, :scalar_columns, :], rows[:, :, :scalar_columns])
+    round_and_interleave(nc.vector.tensor_copy, grouped[:, scalar_columns:, :], rows[:, :, scalar_columns:])
+
+
+def quantize(nc, codes, plane, grouped, fmt):
+    nc.vector.quantize_mx(out=codes.bitcast(fmt), scales=plane, in_=grouped.rearrange("p c j -> p (c j)"))
 
 
 def tile_mix_gradient_of_three_branches_pl_kernel(
@@ -61,135 +80,124 @@ def tile_mix_gradient_of_three_branches_pl_kernel(
         ps = ctx.enter_context(tc.psum_pool(name="ps", bufs=1))
         ctx.enter_context(tc.manual_schedule())
 
-        wc_raw = sb.tile([P, 2, 2 * K], U8, align_bytes=64)
-        wb_raw = sb.tile([P, 2 * K], U8, align_bytes=64)
-        wa_raw = sb.tile([P, K], U32, align_bytes=64)
-        planes = sb.tile([P, 6, K], U8, align_bytes=64)
-        staged = sb.tile([16, 6, K], U8, align_bytes=64)
-        wc_s_raw = planes[:, 0:2, :]
-        gc_s = planes[:, 2:4, :]
-        wa_s_raw = planes[:, 4:5, :]
-        wb_s_raw = planes[:, 5:6, :]
+        wc_arrived = sb.tile([P, 2, 2 * K], U8, align_bytes=64)
+        wb_arrived = sb.tile([P, 2 * K], U8, align_bytes=64)
+        wa_arrived = sb.tile([P, K], U32, align_bytes=64)
+        planes = sb.tile([P, PLANES, K], U8, align_bytes=64)
+        staging = sb.tile([STAGE + BLOCKS, PLANES, K], U8, align_bytes=64)
         wc_codes = sb.tile([P, 2, 2 * K], U8, align_bytes=64)
         wb_codes = sb.tile([P, 2 * K], U8, align_bytes=64)
         wa_codes = sb.tile([P, K], U32, align_bytes=64)
-        wc_s = sb.tile([P, 2, K], U8, align_bytes=64)
-        wb_s = sb.tile([P, 1, K], U8, align_bytes=64)
-        wa_s = sb.tile([P, 1, K], U8, align_bytes=64)
+        wc_plane = sb.tile([P, 2, K], U8, align_bytes=64)
+        wb_plane = sb.tile([P, K], U8, align_bytes=64)
+        wa_plane = sb.tile([P, K], U8, align_bytes=64)
         gc_codes = sb.tile([P, 2, T], U32, align_bytes=64)
-        ga_raw = sb.tile([P, PACK, T], F32, align_bytes=64)
-        gb_raw = [sb.tile([P, PACK, HALF], F32, align_bytes=64, name="gb_raw%d" % h) for h in range(2)]
-        ga_bf = [sb.tile([P, HALF, PACK], BF16, align_bytes=64, name="ga_bf%d" % h) for h in range(2)]
-        gb_bf = [sb.tile([P, HALF, PACK], BF16, align_bytes=64, name="gb_bf%d" % h) for h in range(2)]
-        y_bf = [sb.tile([P, HALF, PACK], BF16, align_bytes=64, name="y_bf%d" % h) for h in range(2)]
+        ga_rows = sb.tile([P, PACK, T], F32, align_bytes=64)
+        gb_rows = [sb.tile([P, PACK, HALF], F32, align_bytes=64, name="gb_rows%d" % h) for h in range(2)]
+        ga_grouped = [sb.tile([P, HALF, PACK], BF16, align_bytes=64, name="ga_grouped%d" % h) for h in range(2)]
+        gb_grouped = [sb.tile([P, HALF, PACK], BF16, align_bytes=64, name="gb_grouped%d" % h) for h in range(2)]
+        y_grouped = [sb.tile([P, HALF, PACK], BF16, align_bytes=64, name="y_grouped%d" % h) for h in range(2)]
         ga_codes = sb.tile([P, T], U32, align_bytes=64)
-        ga_s = sb.tile([P, T], U8, align_bytes=64)
+        ga_plane = sb.tile([P, T], U8, align_bytes=64)
         gb_codes = sb.tile([P, T], U32, align_bytes=64)
-        gb_s = sb.tile([P, T], U8, align_bytes=64)
+        gb_plane = sb.tile([P, T], U8, align_bytes=64)
         y_codes = sb.tile([P, T], U32, align_bytes=64)
-        y_s = sb.tile([P, T], U8, align_bytes=64)
-        y = sb.tile([P, PACK, T], F32, align_bytes=64)
-        fo_sb = sb.tile([P, PACK], F32, align_bytes=64)
-        acc = [ps.tile([P, T], F32, name="acc%d" % r) for r in range(PACK)]
+        y_plane = sb.tile([P, T], U8, align_bytes=64)
+        y_rows = sb.tile([P, PACK, T], F32, align_bytes=64)
+        factors = sb.tile([P, PACK], F32, align_bytes=64)
+        banks = [ps.tile([P, T], F32, name="bank%d" % r) for r in range(PACK)]
 
+        whole = slice(0, T)
         halves = [slice(0, HALF), slice(HALF, T)]
+
+        wc_at, gc_at, wa_at, wb_at = 0, 2, 4, 5
 
         nc.vector.memset(planes[:].bitcast(I32), 0)
 
-        gb_rows = gb.rearrange("(p j) t -> p j t", j=PACK)
-        load_scale_rows(nc.sync, staged[:, 0:2, :], wc_scales)
-        load_scale_rows(nc.sync, staged[:, 2:4, :], gc_scales)
-        load_scale_rows(nc.sync, staged[:, 4:5, :], wa_scales)
-        load_scale_rows(nc.sync, staged[:, 5:6, :], wb_scales)
-        nc.sync.dma_start(out=wc_raw[:].bitcast(I32), in_=wc_words.rearrange("z p b -> p z b").bitcast(I32))
-        nc.sync.dma_start(out=gc_codes[:].bitcast(I32), in_=gc_words.rearrange("z p c r -> p z (c r)").bitcast(I32))
-        nc.sync.dma_start(out=wa_raw[:].bitcast(I32), in_=wa_words[0].rearrange("p c r -> p (c r)").bitcast(I32))
-        nc.sync.dma_start(out=wb_raw[:].bitcast(I32), in_=wb_words[0].bitcast(I32))
-        for q in range(4):
-            nc.sync.dma_start(out=planes[32 * q : 32 * q + 4, :, :].bitcast(I32),
-                              in_=staged[4 * q : 4 * q + 4, :, :].bitcast(I32))
-        nc.sync.dma_start(out=ga_raw[:], in_=ga.rearrange("(p j) t -> p j t", j=PACK))
-        nc.sync.dma_start(out=gb_raw[0][:], in_=gb_rows[:, :, halves[0]])
-        nc.sync.dma_start(out=fo_sb[:], in_=fo.rearrange("(p r) o -> p (r o)", r=PACK))
-        nc.sync.dma_start(out=gb_raw[1][:], in_=gb_rows[:, :, halves[1]])
+        staged = staging[STAGE : STAGE + BLOCKS, :, :]
+        stage_scale_rows(nc.sync, staged[:, wc_at : wc_at + 2, :], wc_scales)
+        stage_scale_rows(nc.sync, staged[:, gc_at : gc_at + 2, :], gc_scales)
+        stage_scale_rows(nc.scalar, staged[:, wa_at : wa_at + 1, :], wa_scales)
+        stage_scale_rows(nc.scalar, staged[:, wb_at : wb_at + 1, :], wb_scales)
+        nc.sync.dma_start(out=wc_arrived[:].bitcast(I32), in_=wc_words.rearrange("z p b -> p z b").bitcast(I32))
+        nc.sync.dma_start(out=wa_arrived[:].bitcast(I32), in_=wa_words[0].rearrange("p c j -> p (c j)").bitcast(I32))
+        nc.sync.dma_start(out=wb_arrived[:].bitcast(I32), in_=wb_words[0].bitcast(I32))
+        nc.sync.dma_start(out=gc_codes[:].bitcast(I32), in_=gc_words.rearrange("z p c j -> p z (c j)").bitcast(I32))
+        for i in range(4):
+            nc.sync.dma_start(
+                out=planes[i:P:QUADRANT, :, :].bitcast(I32),
+                in_=staging[STAGE + i : STAGE + BLOCKS : 4, :, :].bitcast(I32),
+            )
+        nc.sync.dma_start(out=ga_rows[:], in_=ga.rearrange("(p j) t -> p j t", j=PACK))
+        for h in range(2):
+            nc.sync.dma_start(out=gb_rows[h][:], in_=gb.rearrange("(p j) t -> p j t", j=PACK)[:, :, halves[h]])
+        nc.sync.dma_start(out=factors[:], in_=fo.rearrange("(p r) o -> p (r o)", r=PACK))
 
-        def multiply(r, w_codes, w_s, g_codes, g_s, cols, start, stop):
+        def multiply(r, w_codes, w_plane, g_codes, g_plane, cols, start, stop):
             nc.tensor.matmul_mx(
-                out=acc[r][:, cols], lhsT=w_codes, lhsT_scale=w_s[:, r * P : (r + 1) * P],
-                rhs=g_codes, rhs_scale=g_s, start=start, stop=stop,
+                out=banks[r][:, cols], lhsT=w_codes, lhsT_scale=w_plane[:, r * P : (r + 1) * P],
+                rhs=g_codes, rhs_scale=g_plane, start=start, stop=stop,
             )
 
+        def e2m1_hand(codes, r):
+            return codes[:, 2 * P * r : 2 * P * (r + 1)].bitcast(E2M1)
+
         for z in range(2):
-            deal_e2m1(nc, wc_codes[:, z, :], wc_raw[:, z, :])
-        nc.vector.tensor_copy(
-            out=wa_codes[:].bitcast(I32).rearrange("p (r g i) -> p g r i", r=PACK, i=LINE),
-            in_=wa_raw[:].bitcast(I32).rearrange("p (g i r) -> p g r i", r=PACK, i=LINE),
-        )
-        deal_e2m1(nc, wb_codes[:], wb_raw[:])
+            deal_e2m1(nc, wc_codes[:, z, :], wc_arrived[:, z, :])
+        deal_e4m3(nc, wa_codes[:], wa_arrived[:])
+        deal_e2m1(nc, wb_codes[:], wb_arrived[:])
+
         for z in range(2):
-            deal_scales(nc, wc_s[:, z : z + 1, :], wc_s_raw[:, z : z + 1, :])
+            deal_plane(nc, wc_plane[:, z, :], planes[:, wc_at + z, :])
             for r in range(PACK):
-                multiply(r, wc_codes[:, z, 2 * P * r : 2 * P * (r + 1)].bitcast(E2M1), wc_s[:, z, :],
-                         gc_codes[:, z, :].bitcast(E4M3), gc_s[:, z, :], slice(0, T), z == 0, False)
+                multiply(r, e2m1_hand(wc_codes[:, z, :], r), wc_plane[:, z, :],
+                         gc_codes[:, z, :].bitcast(E4M3), planes[:, gc_at + z, :], whole, z == 0, False)
+        deal_plane(nc, wa_plane[:], planes[:, wa_at, :])
+        deal_plane(nc, wb_plane[:], planes[:, wb_at, :])
 
-        deal_scales(nc, wa_s[:], wa_s_raw)
-        deal_scales(nc, wb_s[:], wb_s_raw)
-
-        def round_wide(rows, grouped, share):
-            interleave(nc.scalar.copy, grouped[0][:, :share, :], rows[:, :, :share])
-            interleave(nc.vector.tensor_copy, grouped[1][:], rows[:, :, halves[1]])
-            interleave(nc.vector.tensor_copy, grouped[0][:, share:, :], rows[:, :, share:HALF])
-
-        round_wide(ga_raw, ga_bf, 192)
+        round_and_interleave(nc.scalar.copy, ga_grouped[0][:], ga_rows[:, :, halves[0]])
+        round_and_interleave(nc.vector.tensor_copy, ga_grouped[1][:], ga_rows[:, :, halves[1]])
         for h in (1, 0):
-            quantize(nc, ga_codes[:, halves[h]], ga_s[:, halves[h]], ga_bf[h][:], E5M2)
+            quantize(nc, ga_codes[:, halves[h]], ga_plane[:, halves[h]], ga_grouped[h][:], E5M2)
         for r in range(PACK):
-            multiply(r, wa_codes[:, r * P : (r + 1) * P].bitcast(E4M3), wa_s[:, 0, :],
-                     ga_codes[:].bitcast(E5M2), ga_s[:], slice(0, T), False, False)
+            multiply(r, wa_codes[:, r * P : (r + 1) * P].bitcast(E4M3), wa_plane[:],
+                     ga_codes[:].bitcast(E5M2), ga_plane[:], whole, False, False)
 
         for h in range(2):
-            share = 128 if h == 0 else 96
-            interleave(nc.scalar.copy, gb_bf[h][:, :share, :], gb_raw[h][:, :, :share])
-            interleave(nc.vector.tensor_copy, gb_bf[h][:, share:, :], gb_raw[h][:, :, share:])
-            quantize(nc, gb_codes[:, halves[h]], gb_s[:, halves[h]], gb_bf[h][:], E4M3)
-            for r in range(PACK):
-                for c0 in range(h * HALF, (h + 1) * HALF, NARROW):
-                    cols = slice(c0, c0 + NARROW)
-                    multiply(r, wb_codes[:, 2 * P * r : 2 * P * (r + 1)].bitcast(E2M1), wb_s[:, 0, :],
-                             gb_codes[:, cols].bitcast(E4M3), gb_s[:, cols], cols, False, c0 + NARROW == T)
+            round_on_both_engines(nc, gb_grouped[h], gb_rows[h], SCALAR_COLUMNS_GB)
+        for h in range(2):
+            quantize(nc, gb_codes[:, halves[h]], gb_plane[:, halves[h]], gb_grouped[h][:], E4M3)
+            for r in (0, 1):
+                for first in range(h * HALF, (h + 1) * HALF, NARROW):
+                    cols = slice(first, first + NARROW)
+                    multiply(r, e2m1_hand(wb_codes, r), wb_plane[:], gb_codes[:, cols].bitcast(E4M3),
+                             gb_plane[:, cols], cols, False, first + NARROW == T)
+        for r in (3, 2):
+            multiply(r, e2m1_hand(wb_codes, r), wb_plane[:], gb_codes[:].bitcast(E4M3), gb_plane[:], whole, False, True)
 
-        out_rows = out_0.rearrange("(p r) t -> p r t", r=PACK)
         def scale_on_scalar(r, cols):
-            nc.scalar.activation(out=y[:, r, cols], in_=acc[r][:, cols], func=mybir.ActivationFunctionType.Copy,
-                                 scale=fo_sb[:, r : r + 1])
+            nc.scalar.activation(out=y_rows[:, r, cols], in_=banks[r][:, cols],
+                                 func=mybir.ActivationFunctionType.Copy, scale=factors[:, r : r + 1])
 
         def scale_on_vector(r, cols):
-            nc.vector.tensor_scalar(out=y[:, r, cols], in0=acc[r][:, cols], scalar1=fo_sb[:, r : r + 1], scalar2=None,
-                                    op0=mybir.AluOpType.mult)
+            nc.vector.tensor_scalar(out=y_rows[:, r, cols], in0=banks[r][:, cols], scalar1=factors[:, r : r + 1],
+                                    scalar2=None, op0=mybir.AluOpType.mult)
 
-        def store_rows(r):
-            nc.sync.dma_start(out=out_rows[:, r, :], in_=y[:, r, :])
-
-        whole = slice(0, T)
-        words = out_1[0].rearrange("p c r -> p (c r)").bitcast(I32)
+        out_rows = out_0.rearrange("(p r) t -> p r t", r=PACK)
         scale_on_scalar(0, whole)
-        store_rows(0)
         scale_on_vector(1, whole)
-        store_rows(1)
+        nc.sync.dma_start(out=out_rows[:, 0:2, :], in_=y_rows[:, 0:2, :])
         scale_on_scalar(2, halves[1])
         scale_on_vector(3, halves[1])
         scale_on_scalar(2, halves[0])
-        store_rows(2)
         scale_on_scalar(3, halves[0])
-        store_rows(3)
-        share = 192
-        interleave(nc.vector.tensor_copy, y_bf[1][:], y[:, :, halves[1]])
-        interleave(nc.scalar.copy, y_bf[0][:, :share, :], y[:, :, :share])
-        interleave(nc.vector.tensor_copy, y_bf[0][:, share:, :], y[:, :, share:HALF])
+        nc.sync.dma_start(out=out_rows[:, 2:4, :], in_=y_rows[:, 2:4, :])
+
+        round_and_interleave(nc.vector.tensor_copy, y_grouped[1][:], y_rows[:, :, halves[1]])
+        round_on_both_engines(nc, y_grouped[0], y_rows[:, :, halves[0]], SCALAR_COLUMNS_Y)
         for h in (1, 0):
-            quantize(nc, y_codes[:, halves[h]], y_s[:, halves[h]], y_bf[h][:], E4M3)
-            nc.sync.dma_start(out=words[:, halves[h]], in_=y_codes[:, halves[h]].bitcast(I32))
-        for q in range(4):
-            queue = nc.scalar if q % 2 == 0 else nc.sync
-            queue.dma_start(out=out_2[0, 4 * q : 4 * q + 4, :].bitcast(I32),
-                            in_=y_s[32 * q : 32 * q + 4, :].bitcast(I32))
+            quantize(nc, y_codes[:, halves[h]], y_plane[:, halves[h]], y_grouped[h][:], E4M3)
+        nc.sync.dma_start(out=out_1[0].rearrange("p c j -> p (c j)").bitcast(I32), in_=y_codes[:].bitcast(I32))
+        for i in range(4):
+            queue = nc.scalar if i % 2 == 0 else nc.sync
+            queue.dma_start(out=out_2[0, i:BLOCKS:4, :].bitcast(I32), in_=y_plane[i:P:QUADRANT, :].bitcast(I32))

from contextlib import ExitStack

import concourse.mybir as mybir

F32 = mybir.dt.float32
BF16 = mybir.dt.bfloat16
I32 = mybir.dt.int32
U32 = mybir.dt.uint32
U8 = mybir.dt.uint8
E4M3 = mybir.dt.float8_e4m3fn_x4
E5M2 = mybir.dt.float8_e5m2_x4
E2M1 = mybir.dt.float4_e2m1fn_x4

P = 128
PACK = 4
T = 512
K = 512
HALF = T // 2
NARROW = 128
LINE = 4
BLOCKS = 16
QUADRANT = 32
STAGE = 16
PLANES = 6

SCALAR_COLUMNS_GB = 96
SCALAR_COLUMNS_Y = 128

FLOPS = 2 * K * T * (512 + 512 + 1024)


def stage_scale_rows(queue, staged, scales):
    queue.dma_start(out=staged.bitcast(I32), in_=scales.rearrange("z q c -> q z c").bitcast(I32))


def deal_plane(nc, dealt, arrived):
    nc.vector.tensor_copy(
        out=dealt.rearrange("p (r m) -> p r m", r=PACK),
        in_=arrived.rearrange("p (m r) -> p r m", r=PACK),
    )


def deal_e2m1(nc, dealt, arrived):
    nc.vector.tensor_copy(
        out=dealt.rearrange("p (r m b) -> p r m b", r=PACK, b=2),
        in_=arrived.rearrange("p (m r b) -> p r m b", r=PACK, b=2),
    )


def deal_e4m3(nc, dealt, arrived):
    nc.vector.tensor_copy(
        out=dealt.bitcast(I32).rearrange("p (r g i) -> p g r i", r=PACK, i=LINE),
        in_=arrived.bitcast(I32).rearrange("p (g i r) -> p g r i", r=PACK, i=LINE),
    )


def round_and_interleave(copy, grouped, rows):
    copy(
        out=grouped.rearrange("p (c i) j -> p c j i", i=LINE),
        in_=rows.rearrange("p j (c i) -> p c j i", i=LINE),
    )


def round_on_both_engines(nc, grouped, rows, scalar_columns):
    round_and_interleave(nc.scalar.copy, grouped[:, :scalar_columns, :], rows[:, :, :scalar_columns])
    round_and_interleave(nc.vector.tensor_copy, grouped[:, scalar_columns:, :], rows[:, :, scalar_columns:])


def quantize(nc, codes, plane, grouped, fmt):
    nc.vector.quantize_mx(out=codes.bitcast(fmt), scales=plane, in_=grouped.rearrange("p c j -> p (c j)"))


def tile_mix_gradient_of_three_branches_pl_kernel(
    tc, ga, wa_words, wa_scales, gb, wb_words, wb_scales, gc_words, gc_scales, wc_words, wc_scales, fo,
    out_0, out_1, out_2,
):
    nc = tc.nc
    with ExitStack() as ctx:
        sb = ctx.enter_context(tc.tile_pool(name="sb", bufs=1))
        ps = ctx.enter_context(tc.psum_pool(name="ps", bufs=1))
        ctx.enter_context(tc.manual_schedule())

        wc_arrived = sb.tile([P, 2, 2 * K], U8, align_bytes=64)
        wb_arrived = sb.tile([P, 2 * K], U8, align_bytes=64)
        wa_arrived = sb.tile([P, K], U32, align_bytes=64)
        planes = sb.tile([P, PLANES, K], U8, align_bytes=64)
        staging = sb.tile([STAGE + BLOCKS, PLANES, K], U8, align_bytes=64)
        wc_codes = sb.tile([P, 2, 2 * K], U8, align_bytes=64)
        wb_codes = sb.tile([P, 2 * K], U8, align_bytes=64)
        wa_codes = sb.tile([P, K], U32, align_bytes=64)
        wc_plane = sb.tile([P, 2, K], U8, align_bytes=64)
        wb_plane = sb.tile([P, K], U8, align_bytes=64)
        wa_plane = sb.tile([P, K], U8, align_bytes=64)
        gc_codes = sb.tile([P, 2, T], U32, align_bytes=64)
        ga_rows = sb.tile([P, PACK, T], F32, align_bytes=64)
        gb_rows = [sb.tile([P, PACK, HALF], F32, align_bytes=64, name="gb_rows%d" % h) for h in range(2)]
        ga_grouped = [sb.tile([P, HALF, PACK], BF16, align_bytes=64, name="ga_grouped%d" % h) for h in range(2)]
        gb_grouped = [sb.tile([P, HALF, PACK], BF16, align_bytes=64, name="gb_grouped%d" % h) for h in range(2)]
        y_grouped = [sb.tile([P, HALF, PACK], BF16, align_bytes=64, name="y_grouped%d" % h) for h in range(2)]
        ga_codes = sb.tile([P, T], U32, align_bytes=64)
        ga_plane = sb.tile([P, T], U8, align_bytes=64)
        gb_codes = sb.tile([P, T], U32, align_bytes=64)
        gb_plane = sb.tile([P, T], U8, align_bytes=64)
        y_codes = sb.tile([P, T], U32, align_bytes=64)
        y_plane = sb.tile([P, T], U8, align_bytes=64)
        y_rows = sb.tile([P, PACK, T], F32, align_bytes=64)
        factors = sb.tile([P, PACK], F32, align_bytes=64)
        banks = [ps.tile([P, T], F32, name="bank%d" % r) for r in range(PACK)]

        whole = slice(0, T)
        halves = [slice(0, HALF), slice(HALF, T)]

        wc_at, gc_at, wa_at, wb_at = 0, 2, 4, 5

        nc.vector.memset(planes[:].bitcast(I32), 0)

        staged = staging[STAGE : STAGE + BLOCKS, :, :]
        stage_scale_rows(nc.sync, staged[:, wc_at : wc_at + 2, :], wc_scales)
        stage_scale_rows(nc.sync, staged[:, gc_at : gc_at + 2, :], gc_scales)
        stage_scale_rows(nc.scalar, staged[:, wa_at : wa_at + 1, :], wa_scales)
        stage_scale_rows(nc.scalar, staged[:, wb_at : wb_at + 1, :], wb_scales)
        nc.sync.dma_start(out=wc_arrived[:].bitcast(I32), in_=wc_words.rearrange("z p b -> p z b").bitcast(I32))
        nc.sync.dma_start(out=wa_arrived[:].bitcast(I32), in_=wa_words[0].rearrange("p c j -> p (c j)").bitcast(I32))
        nc.sync.dma_start(out=wb_arrived[:].bitcast(I32), in_=wb_words[0].bitcast(I32))
        nc.sync.dma_start(out=gc_codes[:].bitcast(I32), in_=gc_words.rearrange("z p c j -> p z (c j)").bitcast(I32))
        for i in range(4):
            nc.sync.dma_start(
                out=planes[i:P:QUADRANT, :, :].bitcast(I32),
                in_=staging[STAGE + i : STAGE + BLOCKS : 4, :, :].bitcast(I32),
            )
        nc.sync.dma_start(out=ga_rows[:], in_=ga.rearrange("(p j) t -> p j t", j=PACK))
        for h in range(2):
            nc.sync.dma_start(out=gb_rows[h][:], in_=gb.rearrange("(p j) t -> p j t", j=PACK)[:, :, halves[h]])
        nc.sync.dma_start(out=factors[:], in_=fo.rearrange("(p r) o -> p (r o)", r=PACK))

        def multiply(r, w_codes, w_plane, g_codes, g_plane, cols, start, stop):
            nc.tensor.matmul_mx(
                out=banks[r][:, cols], lhsT=w_codes, lhsT_scale=w_plane[:, r * P : (r + 1) * P],
                rhs=g_codes, rhs_scale=g_plane, start=start, stop=stop,
            )

        def e2m1_hand(codes, r):
            return codes[:, 2 * P * r : 2 * P * (r + 1)].bitcast(E2M1)

        for z in range(2):
            deal_e2m1(nc, wc_codes[:, z, :], wc_arrived[:, z, :])
        deal_e4m3(nc, wa_codes[:], wa_arrived[:])
        deal_e2m1(nc, wb_codes[:], wb_arrived[:])

        for z in range(2):
            deal_plane(nc, wc_plane[:, z, :], planes[:, wc_at + z, :])
            for r in range(PACK):
                multiply(r, e2m1_hand(wc_codes[:, z, :], r), wc_plane[:, z, :],
                         gc_codes[:, z, :].bitcast(E4M3), planes[:, gc_at + z, :], whole, z == 0, False)
        deal_plane(nc, wa_plane[:], planes[:, wa_at, :])
        deal_plane(nc, wb_plane[:], planes[:, wb_at, :])

        round_and_interleave(nc.scalar.copy, ga_grouped[0][:], ga_rows[:, :, halves[0]])
        round_and_interleave(nc.vector.tensor_copy, ga_grouped[1][:], ga_rows[:, :, halves[1]])
        for h in (1, 0):
            quantize(nc, ga_codes[:, halves[h]], ga_plane[:, halves[h]], ga_grouped[h][:], E5M2)
        for r in range(PACK):
            multiply(r, wa_codes[:, r * P : (r + 1) * P].bitcast(E4M3), wa_plane[:],
                     ga_codes[:].bitcast(E5M2), ga_plane[:], whole, False, False)

        for h in range(2):
            round_on_both_engines(nc, gb_grouped[h], gb_rows[h], SCALAR_COLUMNS_GB)
        for h in range(2):
            quantize(nc, gb_codes[:, halves[h]], gb_plane[:, halves[h]], gb_grouped[h][:], E4M3)
            for r in (0, 1):
                for first in range(h * HALF, (h + 1) * HALF, NARROW):
                    cols = slice(first, first + NARROW)
                    multiply(r, e2m1_hand(wb_codes, r), wb_plane[:], gb_codes[:, cols].bitcast(E4M3),
                             gb_plane[:, cols], cols, False, first + NARROW == T)
        for r in (3, 2):
            multiply(r, e2m1_hand(wb_codes, r), wb_plane[:], gb_codes[:].bitcast(E4M3), gb_plane[:], whole, False, True)

        def scale_on_scalar(r, cols):
            nc.scalar.activation(out=y_rows[:, r, cols], in_=banks[r][:, cols],
                                 func=mybir.ActivationFunctionType.Copy, scale=factors[:, r : r + 1])

        def scale_on_vector(r, cols):
            nc.vector.tensor_scalar(out=y_rows[:, r, cols], in0=banks[r][:, cols], scalar1=factors[:, r : r + 1],
                                    scalar2=None, op0=mybir.AluOpType.mult)

        out_rows = out_0.rearrange("(p r) t -> p r t", r=PACK)
        scale_on_scalar(0, whole)
        scale_on_vector(1, whole)
        nc.sync.dma_start(out=out_rows[:, 0:2, :], in_=y_rows[:, 0:2, :])
        scale_on_scalar(2, halves[1])
        scale_on_vector(3, halves[1])
        scale_on_scalar(2, halves[0])
        scale_on_scalar(3, halves[0])
        nc.sync.dma_start(out=out_rows[:, 2:4, :], in_=y_rows[:, 2:4, :])

        round_and_interleave(nc.vector.tensor_copy, y_grouped[1][:], y_rows[:, :, halves[1]])
        round_on_both_engines(nc, y_grouped[0], y_rows[:, :, halves[0]], SCALAR_COLUMNS_Y)
        for h in (1, 0):
            quantize(nc, y_codes[:, halves[h]], y_plane[:, halves[h]], y_grouped[h][:], E4M3)
        nc.sync.dma_start(out=out_1[0].rearrange("p c j -> p (c j)").bitcast(I32), in_=y_codes[:].bitcast(I32))
        for i in range(4):
            queue = nc.scalar if i % 2 == 0 else nc.sync
            queue.dma_start(out=out_2[0, i:BLOCKS:4, :].bitcast(I32), in_=y_plane[i:P:QUADRANT, :].bitcast(I32))
